import numpy as np
import ml_dtypes


def mxq(x, axis, fmt="e4m3"):
    dtype, down = {"e4m3": (ml_dtypes.float8_e4m3fn, 7), "e5m2": (ml_dtypes.float8_e5m2, 14)}[fmt]
    v = np.moveaxis(np.asarray(x, np.float32).astype(ml_dtypes.bfloat16).astype(np.float64), axis, -1)
    blocks = v.reshape(v.shape[:-1] + (-1, 32))
    amax = np.abs(blocks).max(-1, keepdims=True)
    byte = np.maximum(np.where(amax > 0, np.frexp(amax)[1] - 1 + 127, 0) - down, 1)
    scale = np.exp2(byte - 127.0)
    codes = (blocks / scale).astype(np.float32).astype(dtype).astype(np.float64)
    return np.moveaxis((codes * scale).reshape(v.shape), -1, axis)


WIDE = False


def mx_kscale(k):
    if not WIDE:
        return np.ones(k)
    levels = np.array([10, -10, 5, -5, 0])
    if k % 512:
        return np.exp2(np.random.permutation(np.resize(levels, k // 32))).repeat(32)
    a = np.empty((k // 512, 16))
    for p in range(k // 512):
        a[p, :8] = np.random.permutation(np.resize(levels, 8))
        for g in range(8):
            far = levels[np.abs(levels - a[p, g]) >= 10]
            a[p, g + 8] = far[np.random.randint(len(far))]
    return np.exp2(a.ravel()).repeat(32)


def f64(x):
    return np.asarray(x).astype(np.float64)


def striped(idx):
    return np.tile(idx.reshape(-1, 16).T, (8, 1)).astype(np.uint16)


def unstriped(offs):
    return offs[:16].T.reshape(-1).astype(np.int64)


def gelu(v):
    return 0.5 * v * (1.0 + np.tanh(np.sqrt(2.0 / np.pi) * (v + 0.044715 * v**3)))


K, T, D, S, V, N = 1024, 2048, 3, 1536, 512, 128
P = 2 ** 7


def setup_inputs():
    n = np.random.standard_normal
    s = mx_kscale(K)[:, None]
    return {
        "xT": (n((K, T)) * s / np.sqrt(D)).astype(ml_dtypes.bfloat16).astype(np.float32),
        "w": (n((K, N)) / np.sqrt(K) / s).astype(np.float32),
        "b": (0.3 * n((N, 1))).astype(np.float32),
        "gate": np.tile(np.random.uniform(0.5, 1.5, (D, 1, V)), (1, P, 1)).astype(ml_dtypes.bfloat16).astype(np.float32),
        "offs": striped(np.concatenate([np.random.permutation(T)[:V] for _ in range(D)])),
    }


def reference(xT, w, b, gate, offs):
    idx = unstriped(offs)
    x = sum(f64(gate)[d, :1] * f64(xT)[:, idx[d * V:(d + 1) * V]] for d in range(D))
    return gelu((mxq(f64(w), 0, "e4m3").T @ mxq(x, 0, "e4m3")) + f64(b))

@@ -1,0 +1,264 @@
+from contextlib import ExitStack
+
+import concourse.mybir as mybir
+from concourse.masks import make_identity
+
+K, T, D, V, N = 1024, 2048, 3, 512, 128
+FLOPS = 2 * K * N * V
+
+F32 = mybir.dt.float32
+BF16 = mybir.dt.bfloat16
+U32 = mybir.dt.uint32
+U16 = mybir.dt.uint16
+U8 = mybir.dt.uint8
+FP8X4 = mybir.dt.float8_e4m3fn_x4
+MULT = mybir.AluOpType.mult
+ADD = mybir.AluOpType.add
+COPY = mybir.ActivationFunctionType.Copy
+GELU = mybir.ActivationFunctionType.Gelu_apprx_tanh
+
+P = 128
+PASSES = 2
+PAIRS = 4
+KIND = "CGCG"
+CHUNKS = [[512,512,512,512],[512,512,512,256,256],[512,512,512,512],[512,512,512,512]]
+CAST = ["SVSV","SSSSS","VVVV","SSSS"]
+CAST_AHEAD = [[0,0,0,0],[0,3,6,2,5],[4,3,2,1],[5,1,4,2]]
+SPAN = [2,4,2,2]
+MUL = [["SSSS","SSSS","SSSS"],["SSSS","SASS","SSSS"],["SSSS","SSSS","SSSS"],["SSVV","SSAA","SSSA"]]
+ROWC = ["VS","SS","SS","SS"]
+OUTC = ["SSSS","VSSS"]
+GATE_CAST = "VVSS"
+W_AFTER = 3
+W_CAST = "SV"
+W_STEP = 20
+LAG = [4,6,8]
+QUANT = [[[0,512]],[[0,256],[256,384],[384,512]]]
+FINISH = [[0,256],[256,384],[384,512]]
+STORE = [[0,384],[384,512]]
+
+
+def tile_picked_bag_lin_gelu_sub_l_kernel(tc, xT, w, b, gate, offs, out):
+    nc = tc.nc
+
+    def cast(engine, dst, src):
+        if engine == "V":
+            nc.vector.tensor_copy(dst, src)
+        elif engine == "S":
+            nc.scalar.copy(dst, src)
+        else:
+            nc.gpsimd.tensor_scalar(dst, src, 1.0, 0.0, MULT, ADD)
+
+    with ExitStack() as ctx:
+        held = ctx.enter_context(tc.tile_pool(name="held", bufs=1))
+        psum = ctx.enter_context(tc.psum_pool(name="psum", bufs=1))
+        offsets = held.tile([P, D * V // 16], U16, name="offsets")
+        sums = [psum.tile([P, 512], F32, name=f"sums{j}") for j in range(4)]
+        ring = [psum.tile([P, 512], F32, name=f"ring{j}") for j in range(4)]
+
+        gate_rows = held.tile([P, D, P], F32, name="gate_rows")
+        gate_cols = held.tile([P, D, 4], F32, name="gate_cols")
+        gate_wide = held.tile([P, D * V], F32, name="gate_wide")
+        bias = held.tile([P, 1], F32, name="bias")
+        zero = held.tile([P, 1], F32, name="zero")
+        warm = held.tile([P, 1], F32, name="warm")
+        ident = held.tile([P, P], F32, name="ident")
+        w_raw = held.tile([P, PASSES, 4, N], F32, name="w_raw")
+        w_bf = held.tile([P, PASSES, N, 4], BF16, name="w_bf", align_bytes=64)
+        w_codes = held.tile([P, PASSES * N], U32, name="w_codes", align_bytes=64)
+        w_scales = held.tile([P, PASSES * N], U8, name="w_scales", align_bytes=64)
+
+        nc.sync.dma_start(gate_rows[0:32], gate.rearrange("d r (c i) -> (r c) d i", c=4)[0:32])
+        nc.vector.memset(zero[:], 0.0)
+        nc.scalar.activation(warm[:], zero[:], GELU)
+        nc.vector.memset(gate_rows[32:64], 0.0)
+        nc.vector.memset(gate_rows[64:128], 0.0)
+        make_identity(nc, ident[:])
+
+        raw = {}
+        for i in range(PAIRS):
+            c, u = divmod(i, 2)
+            rows = xT[512 * c : 512 * (c + 1), :].rearrange("(p t) n -> p t n", t=4)
+            if KIND[i] == "C":
+                for e in range(2):
+                    raw[i, e] = held.tile([P, T], F32, name=f"raw{i}_{e}")
+                    nc.sync.dma_start(raw[i, e][:], rows[:, 2 * u + e, :])
+                    if i == 0 and e == 0:
+                        nc.sync.dma_start(offsets[:], offs)
+            else:
+                n0 = 0
+                for q, width in enumerate(CHUNKS[i]):
+                    raw[i, q] = held.tile([P, 2, width], F32, name=f"raw{i}_{q}")
+                    nc.sync.dma_start(raw[i, q][:], rows[:, 2 * u : 2 * u + 2, n0 : n0 + width])
+                    if i == 0 and q == 0:
+                        nc.sync.dma_start(offsets[:], offs)
+                    n0 += width
+            if i == W_AFTER:
+                nc.sync.dma_start(w_raw[:], w.rearrange("(c p t) n -> p c t n", c=PASSES, t=4))
+        nc.sync.dma_start(bias[:], b)
+
+        window = {i: held.tile([P, T, 2], BF16, name=f"window{i}") for i in range(PAIRS) if KIND[i] == "G"}
+        x_bf = [held.tile([P, V, 4], BF16, name=f"x_bf{c}", align_bytes=64) for c in range(PASSES)]
+        x_codes = [held.tile([P, V], U32, name=f"x_codes{c}", align_bytes=64) for c in range(PASSES)]
+        x_scales = [held.tile([P, V], U8, name=f"x_scales{c}", align_bytes=64) for c in range(PASSES)]
+        result = held.tile([P, V], F32, name="result")
+        parts = {}
+        turn = []
+
+        def next_bank():
+            turn.append(0)
+            return ring[(len(turn) - 1) % 4]
+
+        bank = next_bank()
+        for d in range(D):
+            nc.tensor.transpose(bank[:, d * P : (d + 1) * P], gate_rows[:, d, :], ident[:])
+        cast(GATE_CAST[0], gate_cols[:], bank[:, 0 : D * P].rearrange("p (d r) -> p d r", d=D)[:, :, 0:4])
+        if "C" in KIND:
+            for d in range(D):
+                bank = next_bank()
+                for j in range(4):
+                    nc.tensor.transpose(bank[:, j * P : (j + 1) * P], gate_cols[:, d, j : j + 1].to_broadcast([P, P]), ident[:])
+                cast(GATE_CAST[1 + d], gate_wide[:, d * V : (d + 1) * V], bank[:])
+
+        def cast_chunk(i, q):
+            n0 = sum(CHUNKS[i][:q])
+            cast(CAST[i][q], window[i][:, n0 : n0 + CHUNKS[i][q], :], raw[i, q][:].rearrange("p e n -> p n e"))
+
+        def gather_words(i, j0, nj, d):
+            words = held.tile([P, nj * P], U32, name=f"words{i}_{j0}_{d}")
+            col = (d * V + j0 * P) // 16
+            table = window[i][:].rearrange("p n e -> p (n e)").bitcast(U32)
+            nc.vector.tensor_copy(words[:], table.indirect(offsets[:, col : col + nj * P // 16]))
+            banks = {}
+            for s in range(nj):
+                side = MUL[i][d][j0 + s] == "S"
+                if side not in banks:
+                    banks[side] = next_bank()
+                nc.tensor.transpose(banks[side][:, s * P : (s + 1) * P], words[:, s * P : (s + 1) * P].bitcast(F32), ident[:])
+            return banks
+
+        def weigh(i, j0, nj, d, banks):
+            for s in range(nj):
+                j = j0 + s
+                engine = MUL[i][d][j]
+                src = banks[engine == "S"][:, s * P : (s + 1) * P].bitcast(BF16).rearrange("v (p e) -> v e p", e=2)
+                prod = held.tile([P, 2, P], F32, name=f"prod{i}_{j}_{d}")
+                factor = gate_cols[:, d, j : j + 1]
+                if engine == "S":
+                    nc.scalar.activation(prod[:], src, COPY, scale=factor)
+                elif engine == "V" or (i, j) not in parts:
+                    nc.vector.tensor_scalar(prod[:], src, factor, None, MULT)
+                else:
+                    nc.vector.scalar_tensor_tensor(prod[:], src, factor, parts[i, j].pop()[:], MULT, ADD)
+                parts.setdefault((i, j), []).append(prod)
+
+        def turn_back(i, j):
+            u = i % 2
+            for e in range(2):
+                t = 2 * u + e
+                for r, prod in enumerate(parts[i, j]):
+                    nc.tensor.matmul(sums[j][:, t * P : (t + 1) * P], prod[:, e, :], ident[:], start=(r == 0),
+                                     stop=(r == len(parts[i, j]) - 1), is_transpose=True)
+
+        def gather_row(i, e, d):
+            prod = held.tile([P, V], F32, name=f"rowprod{i}_{e}_{d}")
+            nc.vector.tensor_tensor(prod[:], raw[i, e][:].indirect(offsets[:, d * V // 16 : (d + 1) * V // 16]),
+                                    gate_wide[:, d * V : (d + 1) * V], MULT)
+            parts.setdefault((i, "row", e), []).append(prod)
+
+        def add_row(i, e):
+            bank = next_bank()
+            for j in range(4):
+                for d in range(D):
+                    nc.tensor.matmul(bank[:, j * P : (j + 1) * P], parts[i, "row", e][d][:, j * P : (j + 1) * P], ident[:],
+                                     start=(d == 0), stop=(d == D - 1), is_transpose=True)
+            turned = held.tile([P, V], F32, name=f"turned{i}_{e}")
+            cast(ROWC[i][e], turned[:], bank[:])
+            parts[i, "turned", e] = turned
+
+        def row_back(i, e):
+            t = 2 * (i % 2) + e
+            for j in range(4):
+                nc.tensor.transpose(sums[j][:, t * P : (t + 1) * P], parts[i, "turned", e][:, j * P : (j + 1) * P], ident[:])
+
+        def round_out(c, j):
+            cast(OUTC[c][j], x_bf[c][:, j * P : (j + 1) * P, :], sums[j][:].rearrange("p (t v) -> p v t", t=4))
+
+        def quantize(c, v0, v1):
+            nc.vector.quantize_mx(out=x_codes[c][:, v0:v1].bitcast(FP8X4), scales=x_scales[c][:, v0:v1],
+                                  in_=x_bf[c][:, v0:v1, :].rearrange("p v t -> p (v t)"))
+
+        def finish(v0, v1):
+            bank = next_bank()
+            for c in range(PASSES):
+                nc.tensor.matmul_mx(out=bank[:, 0 : v1 - v0], lhsT=w_codes[:, c * N : (c + 1) * N].bitcast(FP8X4),
+                                    lhsT_scale=w_scales[:, c * N : (c + 1) * N],
+                                    rhs=x_codes[c][:, v0:v1].bitcast(FP8X4), rhs_scale=x_scales[c][:, v0:v1],
+                                    start=(c == 0), stop=(c == PASSES - 1))
+            nc.scalar.activation(result[:, v0:v1], bank[:, 0 : v1 - v0], GELU, bias=bias[:])
+
+        def store(v0, v1):
+            nc.sync.dma_start(out[:, v0:v1], result[:, v0:v1])
+
+        def prepare_w():
+            for c in range(PASSES):
+                cast(W_CAST[c], w_bf[:, c, :, :], w_raw[:, c, :, :].rearrange("p t n -> p n t"))
+
+        def quantize_w():
+            nc.vector.quantize_mx(out=w_codes[:].bitcast(FP8X4), scales=w_scales[:],
+                                  in_=w_bf[:].rearrange("p c n t -> p (c n t)"))
+
+        later = {}
+
+        def at(step, *work):
+            later.setdefault(step, []).extend(work)
+
+        steps = []
+        first = []
+        for i in range(PAIRS):
+            first.append(len(steps))
+            if KIND[i] == "C":
+                steps.extend((i, e, 0, d) for e in range(2) for d in range(D))
+            else:
+                steps.extend((i, j0, SPAN[i], d) for j0 in range(0, 4, SPAN[i]) for d in range(D))
+        for i in range(PAIRS):
+            if KIND[i] == "G":
+                for q in range(len(CHUNKS[i])):
+                    if i == 0:
+                        cast_chunk(i, q)
+                    else:
+                        at(max(0, first[i] - CAST_AHEAD[i][q]), lambda i=i, q=q: cast_chunk(i, q))
+        at(W_STEP, prepare_w)
+        at(W_STEP + 1, quantize_w)
+        for n in range(len(steps) + 8):
+            for work in later.pop(n, []):
+                work()
+            if n >= len(steps):
+                continue
+            i, j0, nj, d = steps[n]
+            c = i // 2
+            if KIND[i] == "C":
+                gather_row(i, j0, d)
+                if d == D - 1:
+                    at(n + 1, lambda i=i, e=j0: add_row(i, e))
+                    at(n + 3, lambda i=i, e=j0: row_back(i, e))
+                continue
+            banks = gather_words(i, j0, nj, d)
+            at(n + 1, lambda i=i, j0=j0, nj=nj, d=d, banks=banks: weigh(i, j0, nj, d, banks))
+            if d < D - 1:
+                continue
+            for j in range(j0, j0 + nj):
+                at(n + LAG[0], lambda i=i, j=j: turn_back(i, j))
+                if i % 2 == 1:
+                    at(n + LAG[1], lambda c=c, j=j: round_out(c, j))
+            if i % 2 == 1:
+                for v0, v1 in QUANT[c]:
+                    if j0 * P < v1 <= (j0 + nj) * P:
+                        at(n + LAG[2], lambda c=c, v0=v0, v1=v1: quantize(c, v0, v1))
+            if i == PAIRS - 1:
+                for v0, v1 in FINISH:
+                    if j0 * P < v1 <= (j0 + nj) * P:
+                        at(n + LAG[2], lambda v0=v0, v1=v1: finish(v0, v1))
+                        for s0, s1 in STORE:
+                            if s1 == v1:
+                                at(n + LAG[2], lambda s0=s0, s1=s1: store(s0, s1))

@@ -20,22 +20,34 @@ GELU = mybir.ActivationFunctionType.Gelu_apprx_tanh
 P = 128
 PASSES = 2
 PAIRS = 4
-KIND = "CGCG"
-CHUNKS = [[512,512,512,512],[512,512,512,256,256],[512,512,512,512],[512,512,512,512]]
-CAST = ["SVSV","SSSSS","VVVV","SSSS"]
-CAST_AHEAD = [[0,0,0,0],[0,3,6,2,5],[4,3,2,1],[5,1,4,2]]
-SPAN = [2,4,2,2]
-MUL = [["SSSS","SSSS","SSSS"],["SSSS","SASS","SSSS"],["SSSS","SSSS","SSSS"],["SSVV","SSAA","SSSA"]]
-ROWC = ["VS","SS","SS","SS"]
-OUTC = ["SSSS","VSSS"]
-GATE_CAST = "VVSS"
+KIND = "GGGG"
+CHUNKS = [[1024,1024],[768,768,512],[768,768,512],[832,832,384]]
+CAST = ["SVS","GGS","GGS","GGS"]
+CAST_AHEAD = [[0,0,0],[6,6,3],[6,6,3],[6,6,3]]
+SPAN = [2,2,2,2]
+MUL = [["SSSS","SSSS","AASS"],["SSSS","SSSS","AASS"],["SSSS","AASS","AASS"],["SSSS","SSAA","AAAA"]]
+ROWC = ["SS","SS","SS","SS"]
+OUTC = ["SSSS","SSSV"]
+GATE_CAST = "SSSV"
 W_AFTER = 3
-W_CAST = "SV"
-W_STEP = 20
-LAG = [4,6,8]
+W_CAST = "SG"
+W_STEP = 22
+LAG = [4,4,4]
 QUANT = [[[0,512]],[[0,256],[256,384],[384,512]]]
 FINISH = [[0,256],[256,384],[384,512]]
-STORE = [[0,384],[384,512]]
+STORE = [[0,256],[256,384],[384,512]]
+WIN = [0,1,2,3]
+ALIAS = [-1,-1,-1,-1,-1,-1,-1,-1,-1,-1,-1,-1,-1,-1,-1,-1,-1,-1,-1,-1,-1,-1,-1,-1,-1,-1,-1,-1,-1,-1]
+W_IN = 19
+GATE_DMA = 0
+LAST = [[0,0,4],[1,0,2],[1,2,1],[1,3,1]]
+ROW_LAG = 2
+END_LAG = [3,3]
+CAST_AFTER = [[-1,-1,-1],[-1,-1,2],[-1,-1,8],[-1,-1,13]]
+DIRECT = "0000"
+EARLY = 0
+PIECES = [[1024,768,256],[768,768,512],[768,768,512],[832,832,384]]
+GATHER_AFTER = [-1,-1,-1,-1,-1,-1,-1,-1,-1,-1,-1,-1,-1,-1,-1,-1,-1,-1,-1,-1,-1,-1,-1,-1,-1,-1,-1,-1,-1,-1]
 
 
 def tile_picked_bag_lin_gelu_sub_l_kernel(tc, xT, w, b, gate, offs, out):
@@ -58,13 +70,13 @@ def tile_picked_bag_lin_gelu_sub_l_kernel(tc, xT, w, b, gate, offs, out):
 
         gate_rows = held.tile([P, D, P], F32, name="gate_rows")
         gate_cols = held.tile([P, D, 4], F32, name="gate_cols")
-        gate_wide = held.tile([P, D * V], F32, name="gate_wide")
+        wide = KIND != "GGGG" or DIRECT != "0000"
+        gate_wide = held.tile([P, D * V], F32, name="gate_wide") if wide else None
         bias = held.tile([P, 1], F32, name="bias")
         zero = held.tile([P, 1], F32, name="zero")
         warm = held.tile([P, 1], F32, name="warm")
         ident = held.tile([P, P], F32, name="ident")
         w_raw = held.tile([P, PASSES, 4, N], F32, name="w_raw")
-        w_bf = held.tile([P, PASSES, N, 4], BF16, name="w_bf", align_bytes=64)
         w_codes = held.tile([P, PASSES * N], U32, name="w_codes", align_bytes=64)
         w_scales = held.tile([P, PASSES * N], U8, name="w_scales", align_bytes=64)
 
@@ -75,29 +87,56 @@ def tile_picked_bag_lin_gelu_sub_l_kernel(tc, xT, w, b, gate, offs, out):
         nc.vector.memset(gate_rows[64:128], 0.0)
         make_identity(nc, ident[:])
 
+        if GATE_DMA:
+            nc.sync.dma_start(gate_wide[:, 0:V], gate[0])
         raw = {}
+        if EARLY:
+            raw[3, 0] = held.tile([P, T], F32, name="raw3_0")
+            nc.sync.dma_start(raw[3, 0][:], xT[512:1024, :].rearrange("(p t) n -> p t n", t=4)[:, 2, :])
+            nc.sync.dma_start(offsets[:], offs)
+            if GATE_DMA:
+                for d in range(1, D):
+                    nc.sync.dma_start(gate_wide[:, d * V : (d + 1) * V], gate[d])
         for i in range(PAIRS):
             c, u = divmod(i, 2)
             rows = xT[512 * c : 512 * (c + 1), :].rearrange("(p t) n -> p t n", t=4)
-            if KIND[i] == "C":
+            if KIND[i] != "G":
                 for e in range(2):
+                    if (i, e) in raw:
+                        continue
                     raw[i, e] = held.tile([P, T], F32, name=f"raw{i}_{e}")
                     nc.sync.dma_start(raw[i, e][:], rows[:, 2 * u + e, :])
-                    if i == 0 and e == 0:
+                    if i == 0 and e == 0 and not EARLY:
                         nc.sync.dma_start(offsets[:], offs)
+                        if GATE_DMA:
+                            for d in range(1, D):
+                                nc.sync.dma_start(gate_wide[:, d * V : (d + 1) * V], gate[d])
             else:
                 n0 = 0
                 for q, width in enumerate(CHUNKS[i]):
                     raw[i, q] = held.tile([P, 2, width], F32, name=f"raw{i}_{q}")
                     nc.sync.dma_start(raw[i, q][:], rows[:, 2 * u : 2 * u + 2, n0 : n0 + width])
-                    if i == 0 and q == 0:
+                    if i == 0 and q == 0 and not EARLY:
                         nc.sync.dma_start(offsets[:], offs)
                     n0 += width
             if i == W_AFTER:
                 nc.sync.dma_start(w_raw[:], w.rearrange("(c p t) n -> p c t n", c=PASSES, t=4))
         nc.sync.dma_start(bias[:], b)
 
-        window = {i: held.tile([P, T, 2], BF16, name=f"window{i}") for i in range(PAIRS) if KIND[i] == "G"}
+        tables = {WIN[i]: 0 for i in range(PAIRS) if KIND[i] == "G"}
+        tables = {s: held.tile([P, T, 2], BF16, name=f"window{s}") for s in tables}
+        window = {i: tables[WIN[i]] for i in range(PAIRS) if KIND[i] == "G"}
+        picked = {}
+
+        def landing(n):
+            if n in picked:
+                return picked[n]
+            if ALIAS[n] >= 0:
+                picked[n] = picked[ALIAS[n]]
+            else:
+                picked[n] = held.tile([P, V], F32, name=f"picked{n}", align_bytes=64)
+            return picked[n]
+
         x_bf = [held.tile([P, V, 4], BF16, name=f"x_bf{c}", align_bytes=64) for c in range(PASSES)]
         x_codes = [held.tile([P, V], U32, name=f"x_codes{c}", align_bytes=64) for c in range(PASSES)]
         x_scales = [held.tile([P, V], U8, name=f"x_scales{c}", align_bytes=64) for c in range(PASSES)]
@@ -113,43 +152,94 @@ def tile_picked_bag_lin_gelu_sub_l_kernel(tc, xT, w, b, gate, offs, out):
         for d in range(D):
             nc.tensor.transpose(bank[:, d * P : (d + 1) * P], gate_rows[:, d, :], ident[:])
         cast(GATE_CAST[0], gate_cols[:], bank[:, 0 : D * P].rearrange("p (d r) -> p d r", d=D)[:, :, 0:4])
-        if "C" in KIND:
+        if not GATE_DMA:
             for d in range(D):
+                if KIND == "GGGG" and (d < D - 1 or DIRECT == "0000"):
+                    continue
                 bank = next_bank()
                 for j in range(4):
                     nc.tensor.transpose(bank[:, j * P : (j + 1) * P], gate_cols[:, d, j : j + 1].to_broadcast([P, P]), ident[:])
                 cast(GATE_CAST[1 + d], gate_wide[:, d * V : (d + 1) * V], bank[:])
 
-        def cast_chunk(i, q):
-            n0 = sum(CHUNKS[i][:q])
-            cast(CAST[i][q], window[i][:, n0 : n0 + CHUNKS[i][q], :], raw[i, q][:].rearrange("p e n -> p n e"))
+        def direct(i, j, d):
+            return i == PAIRS - 1 and d == D - 1 and DIRECT[j] != "0"
 
-        def gather_words(i, j0, nj, d):
-            words = held.tile([P, nj * P], U32, name=f"words{i}_{j0}_{d}")
+        def weigh_last(j):
+            nc.vector.tensor_tensor(last_pairs[:, j * P : (j + 1) * P, :] if DIRECT[j] == "1" else padded[:, j + 1], parts["words", j].bitcast(BF16).rearrange("p (v e) -> p v e", e=2),
+                                    gate_wide[:, 2 * V + j * P : 2 * V + (j + 1) * P].unsqueeze(2).to_broadcast([P, P, 2]), MULT)
+
+        def cast_chunk(i, q):
+            assert (i, q) not in unmarked
+            n0 = sum(PIECES[i][:q])
+            dst = window[i][:, n0 : n0 + PIECES[i][q], :]
+            load = max(r for r in range(len(CHUNKS[i])) if sum(CHUNKS[i][:r]) <= n0)
+            m0 = n0 - sum(CHUNKS[i][:load])
+            assert m0 + PIECES[i][q] <= CHUNKS[i][load]
+            src = raw[i, load][:, :, m0 : m0 + PIECES[i][q]].rearrange("p e n -> p n e")
+            if CAST[i][q] == "S" and 0 <= CAST_AFTER[i][q] < 100:
+                nc.scalar.activation(dst, src, COPY, accum_out=picked[CAST_AFTER[i][q]][:, q : q + 1])
+            else:
+                cast(CAST[i][q], dst, src)
+
+        def gather_words(n, i, j0, nj, d):
+            assert n not in unheld
+            words = landing(n)[:, 0 : nj * P]
             col = (d * V + j0 * P) // 16
             table = window[i][:].rearrange("p n e -> p (n e)").bitcast(U32)
-            nc.vector.tensor_copy(words[:], table.indirect(offsets[:, col : col + nj * P // 16]))
+            nc.vector.tensor_copy(words.bitcast(U32), table.indirect(offsets[:, col : col + nj * P // 16]))
             banks = {}
             for s in range(nj):
+                if direct(i, j0 + s, d):
+                    parts["words", j0 + s] = words[:, s * P : (s + 1) * P]
+                    continue
                 side = MUL[i][d][j0 + s] == "S"
                 if side not in banks:
                     banks[side] = next_bank()
-                nc.tensor.transpose(banks[side][:, s * P : (s + 1) * P], words[:, s * P : (s + 1) * P].bitcast(F32), ident[:])
+                nc.tensor.transpose(banks[side][:, s * P : (s + 1) * P], words[:, s * P : (s + 1) * P], ident[:])
             return banks
 
-        def weigh(i, j0, nj, d, banks):
+        marks = {}
+        for i in range(PAIRS):
+            if KIND[i] == "G":
+                for q in range(len(PIECES[i])):
+                    if CAST_AFTER[i][q] >= (100 if CAST[i][q] == "S" else 0):
+                        marks.setdefault(CAST_AFTER[i][q] % 100, []).append((i, q))
+        holds = {}
+        for n2, n1 in enumerate(GATHER_AFTER):
+            if n1 >= 0:
+                holds.setdefault(n1, []).append(n2)
+        unheld = {x for v in holds.values() for x in v}
+        unmarked = {x for v in marks.values() for x in v}
+
+        def weigh(n, i, j0, nj, d, banks):
             for s in range(nj):
                 j = j0 + s
+                if direct(i, j, d):
+                    continue
                 engine = MUL[i][d][j]
                 src = banks[engine == "S"][:, s * P : (s + 1) * P].bitcast(BF16).rearrange("v (p e) -> v e p", e=2)
                 prod = held.tile([P, 2, P], F32, name=f"prod{i}_{j}_{d}")
                 factor = gate_cols[:, d, j : j + 1]
+                extra = {}
+                row = [MUL[i][d][x] for x in range(j0, j0 + nj) if not direct(i, x, d)]
+                if marks.get(n) and (engine != "S" or set(row) == {"S"}):
+                    i2, q2 = marks[n].pop()
+                    unmarked.remove((i2, q2))
+                    n0 = sum(PIECES[i2][:q2])
+                    extra = {"accum_out": window[i2][:].rearrange("p n e -> p (n e)").bitcast(F32)[:, n0 : n0 + 1]}
+                elif holds.get(n) and (engine != "S" or set(row) == {"S"}):
+                    n2 = holds[n].pop()
+                    assert n2 > n
+                    unheld.remove(n2)
+                    extra = {"accum_out": landing(n2)[:, 0:1]}
                 if engine == "S":
-                    nc.scalar.activation(prod[:], src, COPY, scale=factor)
+                    nc.scalar.activation(prod[:], src, COPY, scale=factor, **extra)
+                elif (engine == "V" or (i, j) not in parts) and extra:
+                    nc.vector.tensor_scalar(prod[:], src, factor, 0.0, MULT, ADD, **extra)
                 elif engine == "V" or (i, j) not in parts:
                     nc.vector.tensor_scalar(prod[:], src, factor, None, MULT)
                 else:
-                    nc.vector.scalar_tensor_tensor(prod[:], src, factor, parts[i, j].pop()[:], MULT, ADD)
+                    nc.vector.scalar_tensor_tensor(prod[:], src, factor, parts[i, j].pop()[:], MULT, ADD, **extra)
                 parts.setdefault((i, j), []).append(prod)
 
         def turn_back(i, j):
@@ -160,18 +250,44 @@ def tile_picked_bag_lin_gelu_sub_l_kernel(tc, xT, w, b, gate, offs, out):
                     nc.tensor.matmul(sums[j][:, t * P : (t + 1) * P], prod[:, e, :], ident[:], start=(r == 0),
                                      stop=(r == len(parts[i, j]) - 1), is_transpose=True)
 
-        def gather_row(i, e, d):
-            prod = held.tile([P, V], F32, name=f"rowprod{i}_{e}_{d}")
+        def gather_row(n, i, e, d):
+            prod = landing(n)
             nc.vector.tensor_tensor(prod[:], raw[i, e][:].indirect(offsets[:, d * V // 16 : (d + 1) * V // 16]),
                                     gate_wide[:, d * V : (d + 1) * V], MULT)
             parts.setdefault((i, "row", e), []).append(prod)
 
+        ends = KIND[3] == "D" or "1" in DIRECT
+        last_terms = held.tile([P, 2, V], F32, name="last_terms") if ends else None
+        last_pairs = last_terms[:].rearrange("p t v -> p (t v)").rearrange("p (v e) -> p v e", e=2) if ends else None
+
+        def gather_last(i, e, j0, nj):
+            col = (2 * V + j0 * P) // 16
+            nc.vector.tensor_tensor(last_terms[:, e, j0 * P : (j0 + nj) * P], raw[i, e][:].indirect(offsets[:, col : col + nj * P // 16]),
+                                    gate_wide[:, 2 * V + j0 * P : 2 * V + (j0 + nj) * P], MULT)
+
+        def round_low(j):
+            cast(OUTC[1][j], x_bf[1][:, j * P : (j + 1) * P, 0:2], sums[j][:, 0 : 2 * P].rearrange("p (t v) -> p v t", t=2))
+
+        padded = held.tile([P, 5, P, 2], F32, name="padded") if "2" in DIRECT else None
+        if "2" in DIRECT:
+            nc.vector.memset(padded[:, 0], 0.0)
+
+        def round_high(j):
+            if DIRECT[j] == "2":
+                nc.vector.tensor_tensor(x_bf[1][:, j * P : (j + 1) * P, :].rearrange("p v (u e) -> p v u e", u=2),
+                                        sums[j][:].rearrange("p (u e v) -> p v u e", u=2, e=2),
+                                        padded[:, 0 : j + 2 : j + 1].rearrange("p u v e -> p v u e"), ADD)
+                return
+            nc.vector.tensor_tensor(x_bf[1][:, j * P : (j + 1) * P, 2:4], sums[j][:, 2 * P : 4 * P].rearrange("p (t v) -> p v t", t=2),
+                                    last_terms[:, :, j * P : (j + 1) * P].rearrange("p t v -> p v t") if KIND[3] == "D" else last_pairs[:, j * P : (j + 1) * P, :], ADD)
+
         def add_row(i, e):
             bank = next_bank()
+            terms = parts[i, "row", e]
             for j in range(4):
-                for d in range(D):
-                    nc.tensor.matmul(bank[:, j * P : (j + 1) * P], parts[i, "row", e][d][:, j * P : (j + 1) * P], ident[:],
-                                     start=(d == 0), stop=(d == D - 1), is_transpose=True)
+                for d in range(len(terms)):
+                    nc.tensor.matmul(bank[:, j * P : (j + 1) * P], terms[d][:, j * P : (j + 1) * P], ident[:],
+                                     start=(d == 0), stop=(d == len(terms) - 1), is_transpose=True)
             turned = held.tile([P, V], F32, name=f"turned{i}_{e}")
             cast(ROWC[i][e], turned[:], bank[:])
             parts[i, "turned", e] = turned
@@ -201,12 +317,15 @@ def tile_picked_bag_lin_gelu_sub_l_kernel(tc, xT, w, b, gate, offs, out):
             nc.sync.dma_start(out[:, v0:v1], result[:, v0:v1])
 
         def prepare_w():
+            spot = picked[W_IN] if W_IN >= 0 else held.tile([P, V], F32, name="w_spot", align_bytes=64)
+            w_bf = spot[:].bitcast(BF16).rearrange("p (c n t) -> p c n t", c=PASSES, t=4)
+            parts["w"] = spot
             for c in range(PASSES):
                 cast(W_CAST[c], w_bf[:, c, :, :], w_raw[:, c, :, :].rearrange("p t n -> p n t"))
 
         def quantize_w():
             nc.vector.quantize_mx(out=w_codes[:].bitcast(FP8X4), scales=w_scales[:],
-                                  in_=w_bf[:].rearrange("p c n t -> p (c n t)"))
+                                  in_=parts["w"][:].bitcast(BF16))
 
         later = {}
 
@@ -215,42 +334,73 @@ def tile_picked_bag_lin_gelu_sub_l_kernel(tc, xT, w, b, gate, offs, out):
 
         steps = []
         first = []
+        if EARLY:
+            steps.extend([(3, 0, 0, 0), (3, 0, 0, 1), (3, 0, (0, 4), 2)])
         for i in range(PAIRS):
             first.append(len(steps))
             if KIND[i] == "C":
                 steps.extend((i, e, 0, d) for e in range(2) for d in range(D))
+            elif KIND[i] == "D":
+                steps.extend((i, e, 0, d) for e in range(EARLY, 2) for d in range(D - 1))
+                steps.extend((i, e, (j0, nj), 2) for e, j0, nj in LAST if e >= EARLY)
             else:
                 steps.extend((i, j0, SPAN[i], d) for j0 in range(0, 4, SPAN[i]) for d in range(D))
         for i in range(PAIRS):
             if KIND[i] == "G":
-                for q in range(len(CHUNKS[i])):
-                    if i == 0:
+                for q in range(len(PIECES[i])):
+                    if i == 0 and not EARLY:
                         cast_chunk(i, q)
                     else:
-                        at(max(0, first[i] - CAST_AHEAD[i][q]), lambda i=i, q=q: cast_chunk(i, q))
+                        at(max(0, first[i] - CAST_AHEAD[i][q]) + 0.5, lambda i=i, q=q: cast_chunk(i, q))
         at(W_STEP, prepare_w)
         at(W_STEP + 1, quantize_w)
-        for n in range(len(steps) + 8):
-            for work in later.pop(n, []):
+        for n in range(len(steps) + 12):
+            for work in later.pop(n, []) + later.pop(n + 0.5, []):
                 work()
             if n >= len(steps):
                 continue
             i, j0, nj, d = steps[n]
             c = i // 2
-            if KIND[i] == "C":
-                gather_row(i, j0, d)
-                if d == D - 1:
-                    at(n + 1, lambda i=i, e=j0: add_row(i, e))
-                    at(n + 3, lambda i=i, e=j0: row_back(i, e))
+            if KIND[i] == "D" and d == 2:
+                gather_last(i, j0, nj[0], nj[1])
+                if j0 == 1:
+                    for j in range(nj[0], nj[0] + nj[1]):
+                        at(n + END_LAG[0], lambda j=j: round_high(j))
+                    for v0, v1 in FINISH:
+                        if nj[0] * P < v1 <= (nj[0] + nj[1]) * P:
+                            at(n + END_LAG[1], lambda v0=v0, v1=v1: quantize(1, v0, v1), lambda v0=v0, v1=v1: finish(v0, v1))
+                            for s0, s1 in STORE:
+                                if s1 == v1:
+                                    at(n + END_LAG[1], lambda s0=s0, s1=s1: store(s0, s1))
                 continue
-            banks = gather_words(i, j0, nj, d)
-            at(n + 1, lambda i=i, j0=j0, nj=nj, d=d, banks=banks: weigh(i, j0, nj, d, banks))
+            if KIND[i] != "G":
+                gather_row(n, i, j0, d)
+                if d == (D - 1 if KIND[i] == "C" else D - 2):
+                    at(n + 1, lambda i=i, e=j0: add_row(i, e))
+                    at(first[3] if EARLY and n < 3 else n + (3 if KIND[i] == "C" else ROW_LAG), lambda i=i, e=j0: row_back(i, e))
+                    if i == 2 and j0 == 1:
+                        for j in range(4):
+                            if KIND[3] == "D" or DIRECT[j] == "1":
+                                at(n + 3, lambda j=j: round_low(j))
+                continue
+            banks = gather_words(n, i, j0, nj, d)
+            at(n + 1, lambda n=n, i=i, j0=j0, nj=nj, d=d, banks=banks: weigh(n, i, j0, nj, d, banks))
+            if d == D - 2:
+                for j in range(j0, j0 + nj):
+                    if direct(i, j, D - 1):
+                        at(n + LAG[0], lambda i=i, j=j: turn_back(i, j))
             if d < D - 1:
                 continue
             for j in range(j0, j0 + nj):
+                if direct(i, j, d):
+                    at(n + END_LAG[0], lambda j=j: weigh_last(j))
+                    at(n + LAG[1], lambda j=j: round_high(j))
+                    continue
                 at(n + LAG[0], lambda i=i, j=j: turn_back(i, j))
                 if i % 2 == 1:
                     at(n + LAG[1], lambda c=c, j=j: round_out(c, j))
+                elif i == 2 and (KIND[3] == "D" or DIRECT[j] == "1"):
+                    at(n + LAG[1], lambda j=j: round_low(j))
             if i % 2 == 1:
                 for v0, v1 in QUANT[c]:
                     if j0 * P < v1 <= (j0 + nj) * P:

@@ -20,58 +20,38 @@ GELU = mybir.ActivationFunctionType.Gelu_apprx_tanh
 P = 128
 PASSES = 2
 PAIRS = 4
-KIND = "GGGG"
-CHUNKS = [[1024,1024],[768,768,512],[768,768,512],[832,832,384]]
-CAST = ["SVS","GGS","GGS","GGS"]
-CAST_AHEAD = [[0,0,0],[6,6,3],[6,6,3],[6,6,3]]
-SPAN = [2,2,2,2]
-MUL = [["SSSS","SSSS","AASS"],["SSSS","SSSS","AASS"],["SSSS","AASS","AASS"],["SSSS","SSAA","AAAA"]]
-ROWC = ["SS","SS","SS","SS"]
-OUTC = ["SSSS","SSSV"]
-GATE_CAST = "SSSV"
-W_AFTER = 3
-W_CAST = "SG"
-W_STEP = 22
-LAG = [4,4,4]
-QUANT = [[[0,512]],[[0,256],[256,384],[384,512]]]
-FINISH = [[0,256],[256,384],[384,512]]
-STORE = [[0,256],[256,384],[384,512]]
-WIN = [0,1,2,3]
-ALIAS = [-1,-1,-1,-1,-1,-1,-1,-1,-1,-1,-1,-1,-1,-1,-1,-1,-1,-1,-1,-1,-1,-1,-1,-1,-1,-1,-1,-1,-1,-1]
-W_IN = 19
-GATE_DMA = 0
-LAST = [[0,0,4],[1,0,2],[1,2,1],[1,3,1]]
-ROW_LAG = 2
-END_LAG = [3,3]
-CAST_AFTER = [[-1,-1,-1],[-1,-1,2],[-1,-1,8],[-1,-1,13]]
-DIRECT = "0000"
-EARLY = 0
-PIECES = [[1024,768,256],[768,768,512],[768,768,512],[832,832,384]]
-GATHER_AFTER = [-1,-1,-1,-1,-1,-1,-1,-1,-1,-1,-1,-1,-1,-1,-1,-1,-1,-1,-1,-1,-1,-1,-1,-1,-1,-1,-1,-1,-1,-1]
+BLOCKS = 4
+STEP_WORDS = 256
+PAIR_STEPS = 6
+STEPS = PAIRS * PAIR_STEPS
+LAST_PAIR = PAIRS - 1
+LAST_BLOCK = BLOCKS - 1
+OFFSETS_PER_COLUMN = 16
+
+FIRST_WIDTHS = (576, 576, 576, 320)
+FIRST_ENGINES = ("gpsimd", "gpsimd", "scalar", "vector")
+LATER_WIDTHS = (768, 768, 512)
+VECTOR_STEPS = (2, 3)
+VECTOR_TAIL = ((20, 1), (22, 0), (22, 1), (23, 0))
+FIRST_SUMS_STEPS, LAST_SUMS_STEP, W_STEP = (14, 15), 17, 20
+RING = 3
 
 
 def tile_picked_bag_lin_gelu_sub_l_kernel(tc, xT, w, b, gate, offs, out):
     nc = tc.nc
 
-    def cast(engine, dst, src):
-        if engine == "V":
-            nc.vector.tensor_copy(dst, src)
-        elif engine == "S":
-            nc.scalar.copy(dst, src)
-        else:
-            nc.gpsimd.tensor_scalar(dst, src, 1.0, 0.0, MULT, ADD)
-
     with ExitStack() as ctx:
         held = ctx.enter_context(tc.tile_pool(name="held", bufs=1))
         psum = ctx.enter_context(tc.psum_pool(name="psum", bufs=1))
-        offsets = held.tile([P, D * V // 16], U16, name="offsets")
-        sums = [psum.tile([P, 512], F32, name=f"sums{j}") for j in range(4)]
-        ring = [psum.tile([P, 512], F32, name=f"ring{j}") for j in range(4)]
+        offsets = held.tile([P, D * V // OFFSETS_PER_COLUMN], U16, name="offsets")
+        sums = [psum.tile([P, 4 * P], F32, name=f"sums{j}") for j in range(BLOCKS)]
+        ring = [psum.tile([P, 4 * P], F32, name=f"ring{r}") for r in range(RING)]
+        vector_bank = psum.tile([P, 4 * P], F32, name="vector_bank")
 
         gate_rows = held.tile([P, D, P], F32, name="gate_rows")
-        gate_cols = held.tile([P, D, 4], F32, name="gate_cols")
-        wide = KIND != "GGGG" or DIRECT != "0000"
-        gate_wide = held.tile([P, D * V], F32, name="gate_wide") if wide else None
+        gate_cols = held.tile([P, D, BLOCKS], F32, name="gate_cols")
+        gate_last = held.tile([P, P], F32, name="gate_last")
+        last_term = held.tile([P, 2, P, 2], F32, name="last_term")
         bias = held.tile([P, 1], F32, name="bias")
         zero = held.tile([P, 1], F32, name="zero")
         warm = held.tile([P, 1], F32, name="warm")
@@ -79,336 +59,202 @@ def tile_picked_bag_lin_gelu_sub_l_kernel(tc, xT, w, b, gate, offs, out):
         w_raw = held.tile([P, PASSES, 4, N], F32, name="w_raw")
         w_codes = held.tile([P, PASSES * N], U32, name="w_codes", align_bytes=64)
         w_scales = held.tile([P, PASSES * N], U8, name="w_scales", align_bytes=64)
+        words = held.tile([P, STEPS * STEP_WORDS], F32, name="words", align_bytes=64)
 
-        nc.sync.dma_start(gate_rows[0:32], gate.rearrange("d r (c i) -> (r c) d i", c=4)[0:32])
+        nc.sync.dma_start(gate_rows[0:32], gate.rearrange("d r (j v) -> (r j) d v", j=BLOCKS)[0:32])
         nc.vector.memset(zero[:], 0.0)
         nc.scalar.activation(warm[:], zero[:], GELU)
         nc.vector.memset(gate_rows[32:64], 0.0)
         nc.vector.memset(gate_rows[64:128], 0.0)
         make_identity(nc, ident[:])
 
-        if GATE_DMA:
-            nc.sync.dma_start(gate_wide[:, 0:V], gate[0])
+        widths = [FIRST_WIDTHS] + [LATER_WIDTHS] * LAST_PAIR
         raw = {}
-        if EARLY:
-            raw[3, 0] = held.tile([P, T], F32, name="raw3_0")
-            nc.sync.dma_start(raw[3, 0][:], xT[512:1024, :].rearrange("(p t) n -> p t n", t=4)[:, 2, :])
-            nc.sync.dma_start(offsets[:], offs)
-            if GATE_DMA:
-                for d in range(1, D):
-                    nc.sync.dma_start(gate_wide[:, d * V : (d + 1) * V], gate[d])
         for i in range(PAIRS):
             c, u = divmod(i, 2)
-            rows = xT[512 * c : 512 * (c + 1), :].rearrange("(p t) n -> p t n", t=4)
-            if KIND[i] != "G":
-                for e in range(2):
-                    if (i, e) in raw:
-                        continue
-                    raw[i, e] = held.tile([P, T], F32, name=f"raw{i}_{e}")
-                    nc.sync.dma_start(raw[i, e][:], rows[:, 2 * u + e, :])
-                    if i == 0 and e == 0 and not EARLY:
-                        nc.sync.dma_start(offsets[:], offs)
-                        if GATE_DMA:
-                            for d in range(1, D):
-                                nc.sync.dma_start(gate_wide[:, d * V : (d + 1) * V], gate[d])
-            else:
-                n0 = 0
-                for q, width in enumerate(CHUNKS[i]):
-                    raw[i, q] = held.tile([P, 2, width], F32, name=f"raw{i}_{q}")
-                    nc.sync.dma_start(raw[i, q][:], rows[:, 2 * u : 2 * u + 2, n0 : n0 + width])
-                    if i == 0 and q == 0 and not EARLY:
-                        nc.sync.dma_start(offsets[:], offs)
-                    n0 += width
-            if i == W_AFTER:
-                nc.sync.dma_start(w_raw[:], w.rearrange("(c p t) n -> p c t n", c=PASSES, t=4))
+            rows = xT[4 * P * c : 4 * P * (c + 1), :].rearrange("(p t) n -> p t n", t=4)
+            for q, width in enumerate(widths[i]):
+                start = sum(widths[i][:q])
+                raw[i, q] = held.tile([P, 2, width], F32, name=f"raw{i}_{q}")
+                nc.sync.dma_start(raw[i, q][:], rows[:, 2 * u : 2 * u + 2, start : start + width])
+                if (i, q) == (0, 0):
+                    nc.sync.dma_start(offsets[:], offs)
+        nc.sync.dma_start(w_raw[:], w.rearrange("(c p t) n -> p c t n", c=PASSES, t=4))
         nc.sync.dma_start(bias[:], b)
+        nc.sync.dma_start(gate_last[:], gate[0][:, LAST_BLOCK * P : V])
+        nc.vector.memset(last_term[:, 0], 0.0)
 
-        tables = {WIN[i]: 0 for i in range(PAIRS) if KIND[i] == "G"}
-        tables = {s: held.tile([P, T, 2], BF16, name=f"window{s}") for s in tables}
-        window = {i: tables[WIN[i]] for i in range(PAIRS) if KIND[i] == "G"}
-        picked = {}
-
-        def landing(n):
-            if n in picked:
-                return picked[n]
-            if ALIAS[n] >= 0:
-                picked[n] = picked[ALIAS[n]]
-            else:
-                picked[n] = held.tile([P, V], F32, name=f"picked{n}", align_bytes=64)
-            return picked[n]
-
+        window = [held.tile([P, T, 2], BF16, name=f"window{i}") for i in range(PAIRS)]
         x_bf = [held.tile([P, V, 4], BF16, name=f"x_bf{c}", align_bytes=64) for c in range(PASSES)]
         x_codes = [held.tile([P, V], U32, name=f"x_codes{c}", align_bytes=64) for c in range(PASSES)]
         x_scales = [held.tile([P, V], U8, name=f"x_scales{c}", align_bytes=64) for c in range(PASSES)]
         result = held.tile([P, V], F32, name="result")
-        parts = {}
-        turn = []
+
+        def step_words(n):
+            return words[:, n * STEP_WORDS : (n + 1) * STEP_WORDS]
+
+        w_bf = words[:, (W_STEP - 2) * STEP_WORDS : W_STEP * STEP_WORDS].bitcast(BF16)
+
+        turns = []
+        turned = {}
+        products = {}
 
         def next_bank():
-            turn.append(0)
-            return ring[(len(turn) - 1) % 4]
+            turns.append(len(turns))
+            return ring[turns[-1] % RING]
+
+        def on_vector(n, s):
+            if n // PAIR_STEPS == LAST_PAIR:
+                return (n, s) in VECTOR_TAIL
+            return n % PAIR_STEPS in VECTOR_STEPS
+
+        def blocks_of(n):
+            return range(1 if n == STEPS - 1 else 2)
 
         bank = next_bank()
         for d in range(D):
             nc.tensor.transpose(bank[:, d * P : (d + 1) * P], gate_rows[:, d, :], ident[:])
-        cast(GATE_CAST[0], gate_cols[:], bank[:, 0 : D * P].rearrange("p (d r) -> p d r", d=D)[:, :, 0:4])
-        if not GATE_DMA:
-            for d in range(D):
-                if KIND == "GGGG" and (d < D - 1 or DIRECT == "0000"):
-                    continue
-                bank = next_bank()
-                for j in range(4):
-                    nc.tensor.transpose(bank[:, j * P : (j + 1) * P], gate_cols[:, d, j : j + 1].to_broadcast([P, P]), ident[:])
-                cast(GATE_CAST[1 + d], gate_wide[:, d * V : (d + 1) * V], bank[:])
+        nc.scalar.activation(gate_cols[:], bank[:, 0 : D * P].rearrange("v (d r) -> v d r", d=D)[:, :, 0:BLOCKS], COPY)
 
-        def direct(i, j, d):
-            return i == PAIRS - 1 and d == D - 1 and DIRECT[j] != "0"
+        def cast_operands(i, q):
+            start = sum(widths[i][:q])
+            return window[i][:, start : start + widths[i][q], :], raw[i, q][:].rearrange("p e n -> p n e")
 
-        def weigh_last(j):
-            nc.vector.tensor_tensor(last_pairs[:, j * P : (j + 1) * P, :] if DIRECT[j] == "1" else padded[:, j + 1], parts["words", j].bitcast(BF16).rearrange("p (v e) -> p v e", e=2),
-                                    gate_wide[:, 2 * V + j * P : 2 * V + (j + 1) * P].unsqueeze(2).to_broadcast([P, P, 2]), MULT)
+        def cast_on_gpsimd(dst, src):
+            nc.gpsimd.tensor_scalar(dst, src, 1.0, 0.0, MULT, ADD)
 
-        def cast_chunk(i, q):
-            assert (i, q) not in unmarked
-            n0 = sum(PIECES[i][:q])
-            dst = window[i][:, n0 : n0 + PIECES[i][q], :]
-            load = max(r for r in range(len(CHUNKS[i])) if sum(CHUNKS[i][:r]) <= n0)
-            m0 = n0 - sum(CHUNKS[i][:load])
-            assert m0 + PIECES[i][q] <= CHUNKS[i][load]
-            src = raw[i, load][:, :, m0 : m0 + PIECES[i][q]].rearrange("p e n -> p n e")
-            if CAST[i][q] == "S" and 0 <= CAST_AFTER[i][q] < 100:
-                nc.scalar.activation(dst, src, COPY, accum_out=picked[CAST_AFTER[i][q]][:, q : q + 1])
-            else:
-                cast(CAST[i][q], dst, src)
-
-        def gather_words(n, i, j0, nj, d):
-            assert n not in unheld
-            words = landing(n)[:, 0 : nj * P]
-            col = (d * V + j0 * P) // 16
-            table = window[i][:].rearrange("p n e -> p (n e)").bitcast(U32)
-            nc.vector.tensor_copy(words.bitcast(U32), table.indirect(offsets[:, col : col + nj * P // 16]))
-            banks = {}
-            for s in range(nj):
-                if direct(i, j0 + s, d):
-                    parts["words", j0 + s] = words[:, s * P : (s + 1) * P]
-                    continue
-                side = MUL[i][d][j0 + s] == "S"
-                if side not in banks:
-                    banks[side] = next_bank()
-                nc.tensor.transpose(banks[side][:, s * P : (s + 1) * P], words[:, s * P : (s + 1) * P], ident[:])
-            return banks
-
-        marks = {}
-        for i in range(PAIRS):
-            if KIND[i] == "G":
-                for q in range(len(PIECES[i])):
-                    if CAST_AFTER[i][q] >= (100 if CAST[i][q] == "S" else 0):
-                        marks.setdefault(CAST_AFTER[i][q] % 100, []).append((i, q))
-        holds = {}
-        for n2, n1 in enumerate(GATHER_AFTER):
-            if n1 >= 0:
-                holds.setdefault(n1, []).append(n2)
-        unheld = {x for v in holds.values() for x in v}
-        unmarked = {x for v in marks.values() for x in v}
-
-        def weigh(n, i, j0, nj, d, banks):
-            for s in range(nj):
-                j = j0 + s
-                if direct(i, j, d):
-                    continue
-                engine = MUL[i][d][j]
-                src = banks[engine == "S"][:, s * P : (s + 1) * P].bitcast(BF16).rearrange("v (p e) -> v e p", e=2)
-                prod = held.tile([P, 2, P], F32, name=f"prod{i}_{j}_{d}")
-                factor = gate_cols[:, d, j : j + 1]
-                extra = {}
-                row = [MUL[i][d][x] for x in range(j0, j0 + nj) if not direct(i, x, d)]
-                if marks.get(n) and (engine != "S" or set(row) == {"S"}):
-                    i2, q2 = marks[n].pop()
-                    unmarked.remove((i2, q2))
-                    n0 = sum(PIECES[i2][:q2])
-                    extra = {"accum_out": window[i2][:].rearrange("p n e -> p (n e)").bitcast(F32)[:, n0 : n0 + 1]}
-                elif holds.get(n) and (engine != "S" or set(row) == {"S"}):
-                    n2 = holds[n].pop()
-                    assert n2 > n
-                    unheld.remove(n2)
-                    extra = {"accum_out": landing(n2)[:, 0:1]}
-                if engine == "S":
-                    nc.scalar.activation(prod[:], src, COPY, scale=factor, **extra)
-                elif (engine == "V" or (i, j) not in parts) and extra:
-                    nc.vector.tensor_scalar(prod[:], src, factor, 0.0, MULT, ADD, **extra)
-                elif engine == "V" or (i, j) not in parts:
-                    nc.vector.tensor_scalar(prod[:], src, factor, None, MULT)
+        def cast_first_pair():
+            for q, engine in enumerate(FIRST_ENGINES):
+                dst, src = cast_operands(0, q)
+                if engine == "gpsimd":
+                    cast_on_gpsimd(dst, src)
+                elif engine == "scalar":
+                    nc.scalar.activation(dst, src, COPY)
                 else:
-                    nc.vector.scalar_tensor_tensor(prod[:], src, factor, parts[i, j].pop()[:], MULT, ADD, **extra)
-                parts.setdefault((i, j), []).append(prod)
+                    nc.vector.tensor_copy(dst, src)
+
+        def gather(n):
+            d, h = D - 1 - n % D, n // D % 2
+            first = (d * V + h * STEP_WORDS) // OFFSETS_PER_COLUMN
+            table = window[n // PAIR_STEPS][:].rearrange("p n e -> p (n e)").bitcast(U32)
+            nc.vector.tensor_copy(step_words(n).bitcast(U32),
+                                  table.indirect(offsets[:, first : first + STEP_WORDS // OFFSETS_PER_COLUMN]))
+
+        def turn_over(n):
+            shared = None
+            for s in blocks_of(n):
+                if on_vector(n, s) and n < STEPS - 1:
+                    place = sum(1 for waiting, column in turned.values() if waiting is vector_bank)
+                    turned[n, s] = (vector_bank, place)
+                else:
+                    if shared is None:
+                        shared = next_bank()
+                    turned[n, s] = (shared, s)
+                target, place = turned[n, s]
+                nc.tensor.transpose(target[:, place * P : (place + 1) * P], step_words(n)[:, s * P : (s + 1) * P], ident[:])
+
+        def weigh(n, s):
+            i, d, j = n // PAIR_STEPS, D - 1 - n % D, 2 * (n // D % 2) + s
+            source, place = turned.pop((n, s))
+            halves = source[:, place * P : (place + 1) * P].bitcast(BF16).rearrange("v (p e) -> v e p", e=2)
+            factor = gate_cols[:, d, j : j + 1]
+            earlier = products.setdefault((i, j), [])
+            if i < LAST_PAIR and (n % PAIR_STEPS, s) == (PAIR_STEPS - 1, 1):
+                product = step_words(PAIR_STEPS * i + 1).rearrange("v (e p) -> v e p", e=2)
+            else:
+                product = held.tile([P, 2, P], F32, name=f"product{n}_{s}")[:]
+            if not on_vector(n, s):
+                nc.scalar.activation(product, halves, COPY, scale=factor)
+            elif n % D > 0:
+                nc.vector.scalar_tensor_tensor(product, halves, factor, earlier.pop(), MULT, ADD)
+            else:
+                nc.vector.tensor_scalar(product, halves, factor, None, MULT)
+            earlier.append(product)
 
         def turn_back(i, j):
-            u = i % 2
+            terms = products[i, j]
             for e in range(2):
-                t = 2 * u + e
-                for r, prod in enumerate(parts[i, j]):
-                    nc.tensor.matmul(sums[j][:, t * P : (t + 1) * P], prod[:, e, :], ident[:], start=(r == 0),
-                                     stop=(r == len(parts[i, j]) - 1), is_transpose=True)
+                t = 2 * (i % 2) + e
+                for r, product in enumerate(terms):
+                    nc.tensor.matmul(sums[j][:, t * P : (t + 1) * P], product[:, e, :], ident[:], start=(r == 0),
+                                     stop=(r == len(terms) - 1), is_transpose=True)
 
-        def gather_row(n, i, e, d):
-            prod = landing(n)
-            nc.vector.tensor_tensor(prod[:], raw[i, e][:].indirect(offsets[:, d * V // 16 : (d + 1) * V // 16]),
-                                    gate_wide[:, d * V : (d + 1) * V], MULT)
-            parts.setdefault((i, "row", e), []).append(prod)
-
-        ends = KIND[3] == "D" or "1" in DIRECT
-        last_terms = held.tile([P, 2, V], F32, name="last_terms") if ends else None
-        last_pairs = last_terms[:].rearrange("p t v -> p (t v)").rearrange("p (v e) -> p v e", e=2) if ends else None
-
-        def gather_last(i, e, j0, nj):
-            col = (2 * V + j0 * P) // 16
-            nc.vector.tensor_tensor(last_terms[:, e, j0 * P : (j0 + nj) * P], raw[i, e][:].indirect(offsets[:, col : col + nj * P // 16]),
-                                    gate_wide[:, 2 * V + j0 * P : 2 * V + (j0 + nj) * P], MULT)
-
-        def round_low(j):
-            cast(OUTC[1][j], x_bf[1][:, j * P : (j + 1) * P, 0:2], sums[j][:, 0 : 2 * P].rearrange("p (t v) -> p v t", t=2))
-
-        padded = held.tile([P, 5, P, 2], F32, name="padded") if "2" in DIRECT else None
-        if "2" in DIRECT:
-            nc.vector.memset(padded[:, 0], 0.0)
-
-        def round_high(j):
-            if DIRECT[j] == "2":
-                nc.vector.tensor_tensor(x_bf[1][:, j * P : (j + 1) * P, :].rearrange("p v (u e) -> p v u e", u=2),
-                                        sums[j][:].rearrange("p (u e v) -> p v u e", u=2, e=2),
-                                        padded[:, 0 : j + 2 : j + 1].rearrange("p u v e -> p v u e"), ADD)
-                return
-            nc.vector.tensor_tensor(x_bf[1][:, j * P : (j + 1) * P, 2:4], sums[j][:, 2 * P : 4 * P].rearrange("p (t v) -> p v t", t=2),
-                                    last_terms[:, :, j * P : (j + 1) * P].rearrange("p t v -> p v t") if KIND[3] == "D" else last_pairs[:, j * P : (j + 1) * P, :], ADD)
-
-        def add_row(i, e):
-            bank = next_bank()
-            terms = parts[i, "row", e]
-            for j in range(4):
-                for d in range(len(terms)):
-                    nc.tensor.matmul(bank[:, j * P : (j + 1) * P], terms[d][:, j * P : (j + 1) * P], ident[:],
-                                     start=(d == 0), stop=(d == len(terms) - 1), is_transpose=True)
-            turned = held.tile([P, V], F32, name=f"turned{i}_{e}")
-            cast(ROWC[i][e], turned[:], bank[:])
-            parts[i, "turned", e] = turned
-
-        def row_back(i, e):
-            t = 2 * (i % 2) + e
-            for j in range(4):
-                nc.tensor.transpose(sums[j][:, t * P : (t + 1) * P], parts[i, "turned", e][:, j * P : (j + 1) * P], ident[:])
+        def round_operands(c, j):
+            return x_bf[c][:, j * P : (j + 1) * P, :], sums[j][:].rearrange("p (t v) -> p v t", t=4)
 
         def round_out(c, j):
-            cast(OUTC[c][j], x_bf[c][:, j * P : (j + 1) * P, :], sums[j][:].rearrange("p (t v) -> p v t", t=4))
+            dst, src = round_operands(c, j)
+            nc.scalar.activation(dst, src, COPY)
 
         def quantize(c, v0, v1):
             nc.vector.quantize_mx(out=x_codes[c][:, v0:v1].bitcast(FP8X4), scales=x_scales[c][:, v0:v1],
                                   in_=x_bf[c][:, v0:v1, :].rearrange("p v t -> p (v t)"))
 
-        def finish(v0, v1):
-            bank = next_bank()
+        def finish(j):
+            v0, v1 = j * P, (j + 1) * P
+            quantize(1, v0, v1)
+            acc = next_bank()[:, 0:P]
             for c in range(PASSES):
-                nc.tensor.matmul_mx(out=bank[:, 0 : v1 - v0], lhsT=w_codes[:, c * N : (c + 1) * N].bitcast(FP8X4),
+                nc.tensor.matmul_mx(out=acc, lhsT=w_codes[:, c * N : (c + 1) * N].bitcast(FP8X4),
                                     lhsT_scale=w_scales[:, c * N : (c + 1) * N],
                                     rhs=x_codes[c][:, v0:v1].bitcast(FP8X4), rhs_scale=x_scales[c][:, v0:v1],
                                     start=(c == 0), stop=(c == PASSES - 1))
-            nc.scalar.activation(result[:, v0:v1], bank[:, 0 : v1 - v0], GELU, bias=bias[:])
+            nc.scalar.activation(result[:, v0:v1], acc, GELU, bias=bias[:])
+            if j % 2 == 1:
+                nc.sync.dma_start(out[:, v0 - P : v1], result[:, v0 - P : v1])
 
-        def store(v0, v1):
-            nc.sync.dma_start(out[:, v0:v1], result[:, v0:v1])
+        cast_first_pair()
+        for n in range(STEPS):
+            i, r = divmod(n, PAIR_STEPS)
+            if r == 0 and i < LAST_PAIR:
+                for q in range(2):
+                    cast_on_gpsimd(*cast_operands(i + 1, q))
+            if r == 2 and i > 0:
+                turn_back(i - 1, 2)
+                turn_back(i - 1, 3)
+            if r == 3 and i < LAST_PAIR:
+                dst, src = cast_operands(i + 1, 2)
+                nc.scalar.activation(dst, src, COPY, accum_out=step_words(PAIR_STEPS * i + 1)[:, 0:1])
+            if r == 4 and i < LAST_PAIR:
+                for m in VECTOR_STEPS:
+                    for s in range(2):
+                        weigh(PAIR_STEPS * i + m, s)
+                turn_back(i, 0)
+                turn_back(i, 1)
+            if n in FIRST_SUMS_STEPS:
+                round_out(0, n - FIRST_SUMS_STEPS[0])
+            if n == LAST_SUMS_STEP:
+                round_out(0, 2)
+                dst, src = round_operands(0, 3)
+                nc.scalar.activation(dst, src, COPY, accum_out=step_words(n - 1)[:, STEP_WORDS - 1 : STEP_WORDS])
+            if n == W_STEP:
+                for c in range(PASSES):
+                    cast_on_gpsimd(w_bf[:, c * 4 * N : (c + 1) * 4 * N].rearrange("p (n t) -> p n t", t=4),
+                                   w_raw[:, c, :, :].rearrange("p t n -> p n t"))
+            gather(n)
+            turn_over(n)
+            for s in range(2):
+                if n > 0 and not on_vector(n - 1, s):
+                    weigh(n - 1, s)
 
-        def prepare_w():
-            spot = picked[W_IN] if W_IN >= 0 else held.tile([P, V], F32, name="w_spot", align_bytes=64)
-            w_bf = spot[:].bitcast(BF16).rearrange("p (c n t) -> p c n t", c=PASSES, t=4)
-            parts["w"] = spot
-            for c in range(PASSES):
-                cast(W_CAST[c], w_bf[:, c, :, :], w_raw[:, c, :, :].rearrange("p t n -> p n t"))
-
-        def quantize_w():
-            nc.vector.quantize_mx(out=w_codes[:].bitcast(FP8X4), scales=w_scales[:],
-                                  in_=parts["w"][:].bitcast(BF16))
-
-        later = {}
-
-        def at(step, *work):
-            later.setdefault(step, []).extend(work)
-
-        steps = []
-        first = []
-        if EARLY:
-            steps.extend([(3, 0, 0, 0), (3, 0, 0, 1), (3, 0, (0, 4), 2)])
-        for i in range(PAIRS):
-            first.append(len(steps))
-            if KIND[i] == "C":
-                steps.extend((i, e, 0, d) for e in range(2) for d in range(D))
-            elif KIND[i] == "D":
-                steps.extend((i, e, 0, d) for e in range(EARLY, 2) for d in range(D - 1))
-                steps.extend((i, e, (j0, nj), 2) for e, j0, nj in LAST if e >= EARLY)
-            else:
-                steps.extend((i, j0, SPAN[i], d) for j0 in range(0, 4, SPAN[i]) for d in range(D))
-        for i in range(PAIRS):
-            if KIND[i] == "G":
-                for q in range(len(PIECES[i])):
-                    if i == 0 and not EARLY:
-                        cast_chunk(i, q)
-                    else:
-                        at(max(0, first[i] - CAST_AHEAD[i][q]) + 0.5, lambda i=i, q=q: cast_chunk(i, q))
-        at(W_STEP, prepare_w)
-        at(W_STEP + 1, quantize_w)
-        for n in range(len(steps) + 12):
-            for work in later.pop(n, []) + later.pop(n + 0.5, []):
-                work()
-            if n >= len(steps):
-                continue
-            i, j0, nj, d = steps[n]
-            c = i // 2
-            if KIND[i] == "D" and d == 2:
-                gather_last(i, j0, nj[0], nj[1])
-                if j0 == 1:
-                    for j in range(nj[0], nj[0] + nj[1]):
-                        at(n + END_LAG[0], lambda j=j: round_high(j))
-                    for v0, v1 in FINISH:
-                        if nj[0] * P < v1 <= (nj[0] + nj[1]) * P:
-                            at(n + END_LAG[1], lambda v0=v0, v1=v1: quantize(1, v0, v1), lambda v0=v0, v1=v1: finish(v0, v1))
-                            for s0, s1 in STORE:
-                                if s1 == v1:
-                                    at(n + END_LAG[1], lambda s0=s0, s1=s1: store(s0, s1))
-                continue
-            if KIND[i] != "G":
-                gather_row(n, i, j0, d)
-                if d == (D - 1 if KIND[i] == "C" else D - 2):
-                    at(n + 1, lambda i=i, e=j0: add_row(i, e))
-                    at(first[3] if EARLY and n < 3 else n + (3 if KIND[i] == "C" else ROW_LAG), lambda i=i, e=j0: row_back(i, e))
-                    if i == 2 and j0 == 1:
-                        for j in range(4):
-                            if KIND[3] == "D" or DIRECT[j] == "1":
-                                at(n + 3, lambda j=j: round_low(j))
-                continue
-            banks = gather_words(n, i, j0, nj, d)
-            at(n + 1, lambda n=n, i=i, j0=j0, nj=nj, d=d, banks=banks: weigh(n, i, j0, nj, d, banks))
-            if d == D - 2:
-                for j in range(j0, j0 + nj):
-                    if direct(i, j, D - 1):
-                        at(n + LAG[0], lambda i=i, j=j: turn_back(i, j))
-            if d < D - 1:
-                continue
-            for j in range(j0, j0 + nj):
-                if direct(i, j, d):
-                    at(n + END_LAG[0], lambda j=j: weigh_last(j))
-                    at(n + LAG[1], lambda j=j: round_high(j))
-                    continue
-                at(n + LAG[0], lambda i=i, j=j: turn_back(i, j))
-                if i % 2 == 1:
-                    at(n + LAG[1], lambda c=c, j=j: round_out(c, j))
-                elif i == 2 and (KIND[3] == "D" or DIRECT[j] == "1"):
-                    at(n + LAG[1], lambda j=j: round_low(j))
-            if i % 2 == 1:
-                for v0, v1 in QUANT[c]:
-                    if j0 * P < v1 <= (j0 + nj) * P:
-                        at(n + LAG[2], lambda c=c, v0=v0, v1=v1: quantize(c, v0, v1))
-            if i == PAIRS - 1:
-                for v0, v1 in FINISH:
-                    if j0 * P < v1 <= (j0 + nj) * P:
-                        at(n + LAG[2], lambda v0=v0, v1=v1: finish(v0, v1))
-                        for s0, s1 in STORE:
-                            if s1 == v1:
-                                at(n + LAG[2], lambda s0=s0, s1=s1: store(s0, s1))
+        nc.vector.quantize_mx(out=w_codes[:].bitcast(FP8X4), scales=w_scales[:], in_=w_bf)
+        for n, s in VECTOR_TAIL:
+            weigh(n, s)
+        turn_back(LAST_PAIR, 0)
+        turn_back(LAST_PAIR, 1)
+        nc.vector.tensor_tensor(last_term[:, 1],
+                                step_words(STEPS - 1)[:, P : 2 * P].bitcast(BF16).rearrange("p (v e) -> p v e", e=2),
+                                gate_last[:].unsqueeze(2).to_broadcast([P, P, 2]), MULT)
+        quantize(0, 0, V // 2)
+        quantize(0, V // 2, V)
+        turn_back(LAST_PAIR, 2)
+        turn_back(LAST_PAIR, 3)
+        round_out(1, 0)
+        round_out(1, 1)
+        finish(0)
+        round_out(1, 2)
+        nc.vector.tensor_tensor(x_bf[1][:, LAST_BLOCK * P : V, :].rearrange("p v (u e) -> p v u e", u=2),
+                                sums[LAST_BLOCK][:].rearrange("p (u e v) -> p v u e", u=2, e=2),
+                                last_term[:].rearrange("p u v e -> p v u e"), ADD)
+        for j in range(1, BLOCKS):
+            finish(j)

from contextlib import ExitStack

import concourse.mybir as mybir
from concourse.masks import make_identity

K, T, D, V, N = 1024, 2048, 3, 512, 128
FLOPS = 2 * K * N * V

F32 = mybir.dt.float32
BF16 = mybir.dt.bfloat16
U32 = mybir.dt.uint32
U16 = mybir.dt.uint16
U8 = mybir.dt.uint8
FP8X4 = mybir.dt.float8_e4m3fn_x4
MULT = mybir.AluOpType.mult
ADD = mybir.AluOpType.add
COPY = mybir.ActivationFunctionType.Copy
GELU = mybir.ActivationFunctionType.Gelu_apprx_tanh

P = 128
PASSES = 2
PAIRS = 4
BLOCKS = 4
STEP_WORDS = 256
PAIR_STEPS = 6
STEPS = PAIRS * PAIR_STEPS
LAST_PAIR = PAIRS - 1
LAST_BLOCK = BLOCKS - 1
OFFSETS_PER_COLUMN = 16

FIRST_WIDTHS = (576, 576, 576, 320)
FIRST_ENGINES = ("gpsimd", "gpsimd", "scalar", "vector")
LATER_WIDTHS = (768, 768, 512)
VECTOR_STEPS = (2, 3)
VECTOR_TAIL = ((20, 1), (22, 0), (22, 1), (23, 0))
FIRST_SUMS_STEPS, LAST_SUMS_STEP, W_STEP = (14, 15), 17, 20
RING = 3


def tile_picked_bag_lin_gelu_sub_l_kernel(tc, xT, w, b, gate, offs, out):
    nc = tc.nc

    with ExitStack() as ctx:
        held = ctx.enter_context(tc.tile_pool(name="held", bufs=1))
        psum = ctx.enter_context(tc.psum_pool(name="psum", bufs=1))
        offsets = held.tile([P, D * V // OFFSETS_PER_COLUMN], U16, name="offsets")
        sums = [psum.tile([P, 4 * P], F32, name=f"sums{j}") for j in range(BLOCKS)]
        ring = [psum.tile([P, 4 * P], F32, name=f"ring{r}") for r in range(RING)]
        vector_bank = psum.tile([P, 4 * P], F32, name="vector_bank")

        gate_rows = held.tile([P, D, P], F32, name="gate_rows")
        gate_cols = held.tile([P, D, BLOCKS], F32, name="gate_cols")
        gate_last = held.tile([P, P], F32, name="gate_last")
        last_term = held.tile([P, 2, P, 2], F32, name="last_term")
        bias = held.tile([P, 1], F32, name="bias")
        zero = held.tile([P, 1], F32, name="zero")
        warm = held.tile([P, 1], F32, name="warm")
        ident = held.tile([P, P], F32, name="ident")
        w_raw = held.tile([P, PASSES, 4, N], F32, name="w_raw")
        w_codes = held.tile([P, PASSES * N], U32, name="w_codes", align_bytes=64)
        w_scales = held.tile([P, PASSES * N], U8, name="w_scales", align_bytes=64)
        words = held.tile([P, STEPS * STEP_WORDS], F32, name="words", align_bytes=64)

        nc.sync.dma_start(gate_rows[0:32], gate.rearrange("d r (j v) -> (r j) d v", j=BLOCKS)[0:32])
        nc.vector.memset(zero[:], 0.0)
        nc.scalar.activation(warm[:], zero[:], GELU)
        nc.vector.memset(gate_rows[32:64], 0.0)
        nc.vector.memset(gate_rows[64:128], 0.0)
        make_identity(nc, ident[:])

        widths = [FIRST_WIDTHS] + [LATER_WIDTHS] * LAST_PAIR
        raw = {}
        for i in range(PAIRS):
            c, u = divmod(i, 2)
            rows = xT[4 * P * c : 4 * P * (c + 1), :].rearrange("(p t) n -> p t n", t=4)
            for q, width in enumerate(widths[i]):
                start = sum(widths[i][:q])
                raw[i, q] = held.tile([P, 2, width], F32, name=f"raw{i}_{q}")
                nc.sync.dma_start(raw[i, q][:], rows[:, 2 * u : 2 * u + 2, start : start + width])
                if (i, q) == (0, 0):
                    nc.sync.dma_start(offsets[:], offs)
        nc.sync.dma_start(w_raw[:], w.rearrange("(c p t) n -> p c t n", c=PASSES, t=4))
        nc.sync.dma_start(bias[:], b)
        nc.sync.dma_start(gate_last[:], gate[0][:, LAST_BLOCK * P : V])
        nc.vector.memset(last_term[:, 0], 0.0)

        window = [held.tile([P, T, 2], BF16, name=f"window{i}") for i in range(PAIRS)]
        x_bf = [held.tile([P, V, 4], BF16, name=f"x_bf{c}", align_bytes=64) for c in range(PASSES)]
        x_codes = [held.tile([P, V], U32, name=f"x_codes{c}", align_bytes=64) for c in range(PASSES)]
        x_scales = [held.tile([P, V], U8, name=f"x_scales{c}", align_bytes=64) for c in range(PASSES)]
        result = held.tile([P, V], F32, name="result")

        def step_words(n):
            return words[:, n * STEP_WORDS : (n + 1) * STEP_WORDS]

        w_bf = words[:, (W_STEP - 2) * STEP_WORDS : W_STEP * STEP_WORDS].bitcast(BF16)

        turns = []
        turned = {}
        products = {}

        def next_bank():
            turns.append(len(turns))
            return ring[turns[-1] % RING]

        def on_vector(n, s):
            if n // PAIR_STEPS == LAST_PAIR:
                return (n, s) in VECTOR_TAIL
            return n % PAIR_STEPS in VECTOR_STEPS

        def blocks_of(n):
            return range(1 if n == STEPS - 1 else 2)

        bank = next_bank()
        for d in range(D):
            nc.tensor.transpose(bank[:, d * P : (d + 1) * P], gate_rows[:, d, :], ident[:])
        nc.scalar.activation(gate_cols[:], bank[:, 0 : D * P].rearrange("v (d r) -> v d r", d=D)[:, :, 0:BLOCKS], COPY)

        def cast_operands(i, q):
            start = sum(widths[i][:q])
            return window[i][:, start : start + widths[i][q], :], raw[i, q][:].rearrange("p e n -> p n e")

        def cast_on_gpsimd(dst, src):
            nc.gpsimd.tensor_scalar(dst, src, 1.0, 0.0, MULT, ADD)

        def cast_first_pair():
            for q, engine in enumerate(FIRST_ENGINES):
                dst, src = cast_operands(0, q)
                if engine == "gpsimd":
                    cast_on_gpsimd(dst, src)
                elif engine == "scalar":
                    nc.scalar.activation(dst, src, COPY)
                else:
                    nc.vector.tensor_copy(dst, src)

        def gather(n):
            d, h = D - 1 - n % D, n // D % 2
            first = (d * V + h * STEP_WORDS) // OFFSETS_PER_COLUMN
            table = window[n // PAIR_STEPS][:].rearrange("p n e -> p (n e)").bitcast(U32)
            nc.vector.tensor_copy(step_words(n).bitcast(U32),
                                  table.indirect(offsets[:, first : first + STEP_WORDS // OFFSETS_PER_COLUMN]))

        def turn_over(n):
            shared = None
            for s in blocks_of(n):
                if on_vector(n, s) and n < STEPS - 1:
                    place = sum(1 for waiting, column in turned.values() if waiting is vector_bank)
                    turned[n, s] = (vector_bank, place)
                else:
                    if shared is None:
                        shared = next_bank()
                    turned[n, s] = (shared, s)
                target, place = turned[n, s]
                nc.tensor.transpose(target[:, place * P : (place + 1) * P], step_words(n)[:, s * P : (s + 1) * P], ident[:])

        def weigh(n, s):
            i, d, j = n // PAIR_STEPS, D - 1 - n % D, 2 * (n // D % 2) + s
            source, place = turned.pop((n, s))
            halves = source[:, place * P : (place + 1) * P].bitcast(BF16).rearrange("v (p e) -> v e p", e=2)
            factor = gate_cols[:, d, j : j + 1]
            earlier = products.setdefault((i, j), [])
            if i < LAST_PAIR and (n % PAIR_STEPS, s) == (PAIR_STEPS - 1, 1):
                product = step_words(PAIR_STEPS * i + 1).rearrange("v (e p) -> v e p", e=2)
            else:
                product = held.tile([P, 2, P], F32, name=f"product{n}_{s}")[:]
            if not on_vector(n, s):
                nc.scalar.activation(product, halves, COPY, scale=factor)
            elif n % D > 0:
                nc.vector.scalar_tensor_tensor(product, halves, factor, earlier.pop(), MULT, ADD)
            else:
                nc.vector.tensor_scalar(product, halves, factor, None, MULT)
            earlier.append(product)

        def turn_back(i, j):
            terms = products[i, j]
            for e in range(2):
                t = 2 * (i % 2) + e
                for r, product in enumerate(terms):
                    nc.tensor.matmul(sums[j][:, t * P : (t + 1) * P], product[:, e, :], ident[:], start=(r == 0),
                                     stop=(r == len(terms) - 1), is_transpose=True)

        def round_operands(c, j):
            return x_bf[c][:, j * P : (j + 1) * P, :], sums[j][:].rearrange("p (t v) -> p v t", t=4)

        def round_out(c, j):
            dst, src = round_operands(c, j)
            nc.scalar.activation(dst, src, COPY)

        def quantize(c, v0, v1):
            nc.vector.quantize_mx(out=x_codes[c][:, v0:v1].bitcast(FP8X4), scales=x_scales[c][:, v0:v1],
                                  in_=x_bf[c][:, v0:v1, :].rearrange("p v t -> p (v t)"))

        def finish(j):
            v0, v1 = j * P, (j + 1) * P
            quantize(1, v0, v1)
            acc = next_bank()[:, 0:P]
            for c in range(PASSES):
                nc.tensor.matmul_mx(out=acc, lhsT=w_codes[:, c * N : (c + 1) * N].bitcast(FP8X4),
                                    lhsT_scale=w_scales[:, c * N : (c + 1) * N],
                                    rhs=x_codes[c][:, v0:v1].bitcast(FP8X4), rhs_scale=x_scales[c][:, v0:v1],
                                    start=(c == 0), stop=(c == PASSES - 1))
            nc.scalar.activation(result[:, v0:v1], acc, GELU, bias=bias[:])
            if j % 2 == 1:
                nc.sync.dma_start(out[:, v0 - P : v1], result[:, v0 - P : v1])

        cast_first_pair()
        for n in range(STEPS):
            i, r = divmod(n, PAIR_STEPS)
            if r == 0 and i < LAST_PAIR:
                for q in range(2):
                    cast_on_gpsimd(*cast_operands(i + 1, q))
            if r == 2 and i > 0:
                turn_back(i - 1, 2)
                turn_back(i - 1, 3)
            if r == 3 and i < LAST_PAIR:
                dst, src = cast_operands(i + 1, 2)
                nc.scalar.activation(dst, src, COPY, accum_out=step_words(PAIR_STEPS * i + 1)[:, 0:1])
            if r == 4 and i < LAST_PAIR:
                for m in VECTOR_STEPS:
                    for s in range(2):
                        weigh(PAIR_STEPS * i + m, s)
                turn_back(i, 0)
                turn_back(i, 1)
            if n in FIRST_SUMS_STEPS:
                round_out(0, n - FIRST_SUMS_STEPS[0])
            if n == LAST_SUMS_STEP:
                round_out(0, 2)
                dst, src = round_operands(0, 3)
                nc.scalar.activation(dst, src, COPY, accum_out=step_words(n - 1)[:, STEP_WORDS - 1 : STEP_WORDS])
            if n == W_STEP:
                for c in range(PASSES):
                    cast_on_gpsimd(w_bf[:, c * 4 * N : (c + 1) * 4 * N].rearrange("p (n t) -> p n t", t=4),
                                   w_raw[:, c, :, :].rearrange("p t n -> p n t"))
            gather(n)
            turn_over(n)
            for s in range(2):
                if n > 0 and not on_vector(n - 1, s):
                    weigh(n - 1, s)

        nc.vector.quantize_mx(out=w_codes[:].bitcast(FP8X4), scales=w_scales[:], in_=w_bf)
        for n, s in VECTOR_TAIL:
            weigh(n, s)
        turn_back(LAST_PAIR, 0)
        turn_back(LAST_PAIR, 1)
        nc.vector.tensor_tensor(last_term[:, 1],
                                step_words(STEPS - 1)[:, P : 2 * P].bitcast(BF16).rearrange("p (v e) -> p v e", e=2),
                                gate_last[:].unsqueeze(2).to_broadcast([P, P, 2]), MULT)
        quantize(0, 0, V // 2)
        quantize(0, V // 2, V)
        turn_back(LAST_PAIR, 2)
        turn_back(LAST_PAIR, 3)
        round_out(1, 0)
        round_out(1, 1)
        finish(0)
        round_out(1, 2)
        nc.vector.tensor_tensor(x_bf[1][:, LAST_BLOCK * P : V, :].rearrange("p v (u e) -> p v u e", u=2),
                                sums[LAST_BLOCK][:].rearrange("p (u e v) -> p v u e", u=2, e=2),
                                last_term[:].rearrange("p u v e -> p v u e"), ADD)
        for j in range(1, BLOCKS):
            finish(j)
